import numpy as np
import ml_dtypes


def mxq(x, axis, fmt="e4m3"):
    dtype, down = {"e4m3": (ml_dtypes.float8_e4m3fn, 7), "e5m2": (ml_dtypes.float8_e5m2, 14)}[fmt]
    v = np.moveaxis(np.asarray(x, np.float32).astype(ml_dtypes.bfloat16).astype(np.float64), axis, -1)
    blocks = v.reshape(v.shape[:-1] + (-1, 32))
    amax = np.abs(blocks).max(-1, keepdims=True)
    byte = np.maximum(np.where(amax > 0, np.frexp(amax)[1] - 1 + 127, 0) - down, 1)
    scale = np.exp2(byte - 127.0)
    codes = (blocks / scale).astype(np.float32).astype(dtype).astype(np.float64)
    return np.moveaxis((codes * scale).reshape(v.shape), -1, axis)


WIDE = False


def mx_kscale(k):
    if not WIDE:
        return np.ones(k)
    levels = np.array([10, -10, 5, -5, 0])
    if k % 512:
        return np.exp2(np.random.permutation(np.resize(levels, k // 32))).repeat(32)
    a = np.empty((k // 512, 16))
    for p in range(k // 512):
        a[p, :8] = np.random.permutation(np.resize(levels, 8))
        for g in range(8):
            far = levels[np.abs(levels - a[p, g]) >= 10]
            a[p, g + 8] = far[np.random.randint(len(far))]
    return np.exp2(a.ravel()).repeat(32)


def f64(x):
    return np.asarray(x).astype(np.float64)


def striped(idx):
    return np.tile(idx.reshape(-1, 16).T, (8, 1)).astype(np.uint16)


def unstriped(offs):
    return offs[:16].T.reshape(-1).astype(np.int64)


E2M1 = np.array([0.0, 0.5, 1.0, 1.5, 2.0, 3.0, 4.0, 6.0, -0.0, -0.5, -1.0, -1.5, -2.0, -3.0, -4.0, -6.0])


def pack_weight(w, fmt):
    k, n = w.shape
    w = f64(np.asarray(w, np.float32).astype(ml_dtypes.bfloat16)).reshape(k // 32, 32, n)
    amax = np.abs(w).max(1)
    if fmt == "e4m3":
        byte = np.frexp(amax)[1] - 1 + 127 - 7
    else:
        mant, ex = np.frexp(amax / 6.0)
        byte = np.where(mant > 0.5, ex, ex - 1) + 127
    byte = np.clip(np.where(amax > 0, byte, 1), 1, 254)
    scaled = (w * np.exp2(127.0 - byte)[:, None, :]).reshape(k, n).astype(np.float32)
    by_word = np.ascontiguousarray(scaled.reshape(k // 512, 128, 4, n).transpose(0, 1, 3, 2))
    if fmt == "e4m3":
        words = by_word.astype(ml_dtypes.float8_e4m3fn).view(np.uint8)
    else:
        c = by_word.astype(ml_dtypes.float4_e2m1fn).view(np.uint8) & 0xF
        words = (c[..., 0::2] | (c[..., 1::2] << 4)).reshape(k // 512, 128, 2 * n)
    return np.ascontiguousarray(words), np.ascontiguousarray(byte.astype(np.uint8).reshape(k // 512, 16, n))


def unpack_weight(words, scales, fmt):
    g, _, n = scales.shape
    words = np.ascontiguousarray(words).reshape(g, 128, n, -1)
    if fmt == "e4m3":
        vals = words.view(ml_dtypes.float8_e4m3fn).astype(np.float64)
    else:
        nib = np.empty((g, 128, n, 4), np.uint8)
        nib[..., 0::2] = words & 0xF
        nib[..., 1::2] = words >> 4
        vals = E2M1[nib]
    vals = vals * np.repeat(np.exp2(scales.astype(np.float64) - 127.0), 8, axis=1)[..., None]
    return vals.transpose(0, 1, 3, 2).reshape(g * 512, n)


def gelu(v):
    return 0.5 * v * (1.0 + np.tanh(np.sqrt(2.0 / np.pi) * (v + 0.044715 * v**3)))


K, KB, KC, H, N, T, S, P = 1536, 512, 1024, 1024, 768, 4096, 1024, 512

def setup_inputs():
    n = np.random.standard_normal
    s = mx_kscale(K)[:, None]
    u = mx_kscale(H)[:, None]
    tab_words, tab_scales = pack_weight(n((K, T)) * s, "e4m3")
    wv_words, wv_scales = pack_weight(n((KB, H)) * 0.9 / np.sqrt(KB) / s[KB:KC], "e2m1")
    wl_words, wl_scales = pack_weight(n((KB, H)) * 0.9 / np.sqrt(KB) / s[KC:], "e4m3")
    wx_words, wx_scales = pack_weight(n((H, N)) / np.sqrt(H) / u, "e2m1")
    return {
        "tab_words": tab_words, "tab_scales": tab_scales,
        "offs": striped(np.random.permutation(T)[:S]),
        "pos1": striped(np.random.permutation(S)[:P]),
        "pos2": striped(np.random.permutation(S)[:P]),
        "wd": (n((KB, H)) * 0.9 / np.sqrt(KB) / s[:KB]).astype(np.float32),
        "wv_words": wv_words, "wv_scales": wv_scales,
        "wl_words": wl_words, "wl_scales": wl_scales,
        "b": (0.6 * n(H)).astype(np.float32),
        "gain": (np.exp(0.3 * n(H)) * u[:, 0]).astype(np.float32),
        "dose": n(H).astype(np.float32),
        "level": (0.8 * n((H, P)) * u).astype(np.float32),
        "wx_words": wx_words, "wx_scales": wx_scales,
        "wm": (n((H, N)) / np.sqrt(H) / u).astype(np.float32),
        "b2": (0.6 * n(N)).astype(np.float32),
    }

def reference(tab_words, tab_scales, offs, pos1, pos2, wd, wv_words, wv_scales, wl_words, wl_scales,
              b, gain, dose, level, wx_words, wx_scales, wm, b2):
    v = unpack_weight(tab_words, tab_scales, "e4m3")[:, unstriped(offs)]
    wv = unpack_weight(wv_words, wv_scales, "e2m1")
    wl = unpack_weight(wl_words, wl_scales, "e4m3")
    wx = unpack_weight(wx_words, wx_scales, "e2m1")
    a = (mxq(f64(wd), 0, "e4m3").T @ v[:KB] + wv.T @ v[KB:KC] + wl.T @ v[KC:]) + f64(b)[:, None]
    h = f64(gain)[:, None] * (a / (1.0 + np.exp(-a)))
    xa = f64(dose)[:, None] * h[:, unstriped(pos1)]
    xb = np.maximum(h[:, unstriped(pos2)], f64(level))
    ya = wx.T @ mxq(xa, 0, "e4m3")
    yb = (mxq(f64(wm), 0, "e4m3").T @ mxq(xb, 0, "e4m3")) + f64(b2)[:, None]
    return np.maximum(ya, yb)

@@ -1,0 +1,331 @@
+from contextlib import ExitStack
+
+import concourse.mybir as mybir
+
+K, KB, H, N, T, S, PICKS = 1536, 512, 1024, 768, 4096, 1024, 512
+FLOPS = 2 * K * H * S + 2 * 2 * H * N * PICKS
+
+F32 = mybir.dt.float32
+BF16 = mybir.dt.bfloat16
+I32 = mybir.dt.int32
+U32 = mybir.dt.uint32
+U16 = mybir.dt.uint16
+U8 = mybir.dt.uint8
+FP8X4 = mybir.dt.float8_e4m3fn_x4
+FP4X4 = mybir.dt.float4_e2m1fn_x4
+ALU = mybir.AluOpType
+SILU = mybir.ActivationFunctionType.Silu
+
+P = 128
+PACK = 4
+BANK = 512
+GROUPS = H // (P * PACK)
+OUT_TILES = N // P
+DRUG, VIAL, DILUENT = 0, 1, 2
+PLANE_ROW = {VIAL: 0, DILUENT: 4, DRUG: 8}
+RUN = 4
+
+
+def tile_list_compounding_release_features_kernel(
+    tc, tab_words, tab_scales, offs, pos1, pos2, wd, wv_words, wv_scales, wl_words, wl_scales,
+    b, gain, dose, level, wx_words, wx_scales, wm, b2, out,
+):
+    nc = tc.nc
+
+    with ExitStack() as ctx:
+        keep = ctx.enter_context(tc.tile_pool(name="keep", bufs=1))
+        ring = ctx.enter_context(tc.tile_pool(name="ring", bufs=1))
+        psum = ctx.enter_context(tc.psum_pool(name="psum", bufs=8))
+
+        def held(shape, dtype, name):
+            return keep.tile(shape, dtype, name=name, align_bytes=64)
+
+        def shared(shape, dtype, tag, bufs, name):
+            return ring.tile(shape, dtype, name=name, tag=tag, bufs=bufs, align_bytes=64)
+
+        def woven(tile):
+            return tile[:].rearrange("p (c i t) -> p c t i", i=RUN, t=PACK)
+
+        def by_rows(tile):
+            return tile[:].rearrange("p t (c i) -> p c t i", i=RUN)
+
+        wv_sc_raw = held([P, H], U8, "wv_sc_raw")
+        wl_sc_raw = held([P, H], U8, "wl_sc_raw")
+        tab_sc = held([P, T], U8, "tab_sc")
+        wx_sc = held([P, GROUPS, N], U8, "wx_sc")
+        nc.vector.memset(tab_sc[:].bitcast(I32), 0)
+        nc.vector.memset(wv_sc_raw[:].bitcast(I32), 0)
+        nc.vector.memset(wl_sc_raw[:].bitcast(I32), 0)
+        nc.vector.memset(wx_sc[:].bitcast(I32), 0)
+
+        def load_channel_vector(vec, name):
+            tile = held([P, GROUPS, 2 * PACK], F32, name)
+            nc.gpsimd.dma_start(out=tile[:, :, 0:PACK], in_=vec.rearrange("(g p t) -> p g t", g=GROUPS, t=PACK))
+            return tile
+
+        def load_list(src, name):
+            tile = held(list(src.shape), U16, name)
+            nc.sync.dma_start(tile[:], src)
+            return tile
+
+        def load_table_half(a, half):
+            words = tab_words[a].rearrange("p t i -> p (t i)").bitcast(I32)
+            cols = slice(half * T // 2, (half + 1) * T // 2)
+            nc.sync.dma_start(out=table[a][:, cols].bitcast(I32), in_=words[:, cols])
+
+        def load_scale_rows(plane, scales, q):
+            nc.sync.dma_start(
+                out=plane[32 * q : 32 * q + 4, :].bitcast(I32), in_=scales[0, 4 * q : 4 * q + 4, :].bitcast(I32)
+            )
+
+        def load_table_scales(q):
+            nc.sync.dma_start(
+                out=tab_sc[32 * q : 32 * q + 8, :].bitcast(I32),
+                in_=tab_scales[VIAL : DILUENT + 1, 4 * q : 4 * q + 4, :].bitcast(I32),
+            )
+            nc.sync.dma_start(
+                out=tab_sc[32 * q + 8 : 32 * q + 12, :].bitcast(I32),
+                in_=tab_scales[DRUG, 4 * q : 4 * q + 4, :].bitcast(I32),
+            )
+
+        def load_wl(g):
+            tile = held([P, BANK], I32, "wl_raw%d" % g)
+            words = wl_words[0].rearrange("p c i -> p (c i)")
+            nc.sync.dma_start(out=tile[:], in_=words[:, g * BANK * PACK : (g + 1) * BANK * PACK].bitcast(I32))
+            return tile
+
+        def load_wd(g):
+            tile = shared([P, PACK, BANK], F32, "mid", 3, "wd_raw%d" % g)
+            nc.sync.dma_start(out=tile[:], in_=wd.rearrange("(p j) c -> p j c", j=PACK)[:, :, g * BANK : (g + 1) * BANK])
+            return tile
+
+        def load_rows(src, g, tag, name):
+            tile = shared([P, PACK, src.shape[1]], F32, tag, 3, name)
+            rows = src[g * P * PACK : (g + 1) * P * PACK, :]
+            nc.sync.dma_start(out=tile[:], in_=rows.rearrange("(p t) c -> p t c", t=PACK))
+            return tile
+
+        table = {a: shared([P, T], U32, "big", 3, "table%d" % a) for a in (VIAL, DILUENT, DRUG)}
+        gain_t = load_channel_vector(gain, "gain_t")
+        dose_t = load_channel_vector(dose, "dose_t")
+        b_t = load_channel_vector(b, "b_t")
+        offs_t = load_list(offs, "offs_t")
+        load_table_half(VIAL, 0)
+        for q in range(3):
+            load_table_scales(q)
+        load_table_half(VIAL, 1)
+        wv_raw = held([P, 2 * H], U8, "wv_raw")
+        nc.sync.dma_start(out=wv_raw[:].bitcast(I32), in_=wv_words[0].bitcast(I32))
+        load_table_scales(3)
+        for q in range(3):
+            load_scale_rows(wv_sc_raw, wv_scales, q)
+        load_table_half(DILUENT, 0)
+        load_scale_rows(wv_sc_raw, wv_scales, 3)
+        wl_raw = [load_wl(0)]
+        for q in range(4):
+            load_scale_rows(wl_sc_raw, wl_scales, q)
+        load_table_half(DILUENT, 1)
+        pos1_t = load_list(pos1, "pos1_t")
+        pos2_t = load_list(pos2, "pos2_t")
+        load_table_half(DRUG, 0)
+        load_table_half(DRUG, 1)
+        wd_raw = [load_wd(0), load_wd(1)]
+        wl_raw.append(load_wl(1))
+        level_t = [load_rows(level, 0, "mid", "level0")]
+        wm_raw = [load_rows(wm, 0, "big", "wm_raw0")]
+        wx_t = held([P, GROUPS, 2 * N], U8, "wx_t")
+        nc.sync.dma_start(out=wx_t[:].bitcast(I32), in_=wx_words.rearrange("a p c -> p a c").bitcast(I32))
+        for q in range(4):
+            nc.sync.dma_start(
+                out=wx_sc[32 * q : 32 * q + 4, :, :].bitcast(I32),
+                in_=wx_scales[:, 4 * q : 4 * q + 4, :].rearrange("a r c -> r a c").bitcast(I32),
+            )
+        wm_raw.append(load_rows(wm, 1, "big", "wm_raw1"))
+        level_t.append(load_rows(level, 1, "mid", "level1"))
+        b2_t = held([P, OUT_TILES], F32, "b2_t")
+        with nc.allow_non_contiguous_dma(reason="one bias value for each partition"):
+            nc.sync.dma_start(out=b2_t[:], in_=b2.rearrange("(u p) -> p u", p=P))
+
+        gain_dose = held([P, GROUPS, PACK], F32, "gain_dose")
+        nc.vector.tensor_tensor(gain_dose[:], gain_t[:, :, 0:PACK], dose_t[:, :, 0:PACK], ALU.mult)
+        factor = {}
+        for g in range(GROUPS):
+            for t in range(PACK):
+                for name, vec in (("a", gain_dose), ("b", gain_t)):
+                    tile = held([P, PICKS], F32, "factor_%s%d%d" % (name, g, t))
+                    nc.scalar.copy(out=tile[:], in_=vec[:, g, t : t + 1].to_broadcast([P, PICKS]))
+                    factor[name, g, t] = tile
+
+        def deal_scales(raw, name):
+            tile = held([P, H], U8, name)
+            nc.vector.tensor_copy(
+                out=tile[:].rearrange("p (g t m) -> p g t m", g=GROUPS, t=PACK),
+                in_=raw[:].rearrange("p (g m t) -> p g t m", g=GROUPS, t=PACK),
+            )
+            return tile
+
+        def deal_wl(g):
+            tile = held([P, PACK, P], I32, "wl_t%d" % g)
+            nc.vector.tensor_copy(out=tile[:], in_=wl_raw[g][:].rearrange("p (m t) -> p t m", t=PACK))
+            return tile
+
+        def gather_table(a):
+            tile = held([P, S], U32, "v%d" % a)
+            nc.vector.tensor_copy(tile[:], table[a][:].indirect(offs_t[:]))
+            return tile
+
+        v = {}
+        v[VIAL] = gather_table(VIAL)
+        wv_sc = deal_scales(wv_sc_raw, "wv_sc")
+        wv_t = held([P, 2 * H], U8, "wv_t")
+        nc.vector.tensor_copy(
+            out=wv_t[:].rearrange("p (g t m e) -> p g t m e", g=GROUPS, t=PACK, e=2),
+            in_=wv_raw[:].rearrange("p (g m t e) -> p g t m e", g=GROUPS, t=PACK, e=2),
+        )
+        v_sc = held([P, S], U8, "v_sc")
+        nc.vector.tensor_copy(v_sc[:], tab_sc[:].indirect(offs_t[:]))
+        v[DILUENT] = gather_table(DILUENT)
+        wl_sc = deal_scales(wl_sc_raw, "wl_sc")
+        wl_t = [deal_wl(0)]
+        v[DRUG] = gather_table(DRUG)
+
+        wd_codes, wd_sc = {}, {}
+
+        def quantise_wd(g, u, cast):
+            rounded = shared([P, 2, P, PACK], BF16, "wd_bf", 2, "wd_bf%d%d" % (g, u))
+            cast(
+                out=rounded[:].rearrange("p e m j -> p m j e"),
+                in_=wd_raw[g][:].rearrange("p j (m u e) -> p u m j e", u=2, e=2)[:, u],
+            )
+            codes = held([P, 2 * P], U32, "wd_codes%d%d" % (g, u))
+            scales = held([P, 2 * P], U8, "wd_sc%d%d" % (g, u))
+            nc.vector.quantize_mx(codes[:].bitcast(FP8X4), scales[:], rounded[:].rearrange("p e m j -> p (e m j)"))
+            for e in range(2):
+                wd_codes[g, 2 * u + e] = codes[:, e * P : (e + 1) * P]
+                wd_sc[g, 2 * u + e] = scales[:, e * P : (e + 1) * P]
+
+        def first_stage_pass(acc, a, g, t, half):
+            cols = slice(half * BANK, (half + 1) * BANK)
+            col0 = (g * PACK + t) * P
+            if a == VIAL:
+                lhsT = wv_t[:, 2 * col0 : 2 * (col0 + P)].bitcast(FP4X4)
+                lhsT_scale = wv_sc[:, col0 : col0 + P]
+            elif a == DILUENT:
+                lhsT = wl_t[g][:, t, :].bitcast(FP8X4)
+                lhsT_scale = wl_sc[:, col0 : col0 + P]
+            else:
+                lhsT = wd_codes[g, t].bitcast(FP8X4)
+                lhsT_scale = wd_sc[g, t]
+            nc.tensor.matmul_mx(
+                out=acc[:], lhsT=lhsT, lhsT_scale=lhsT_scale,
+                rhs=v[a][:, cols].bitcast(FP8X4), rhs_scale=v_sc[PLANE_ROW[a] : P, cols],
+                start=(a == VIAL), stop=(a == DRUG),
+            )
+
+        act = {}
+
+        def finish_tile(g, t, accs):
+            act[g, t] = shared([P, S], F32, "act", 6, "act%d%d" % (g, t))
+            for half in range(2):
+                first_stage_pass(accs[half], DRUG, g, t, half)
+                nc.scalar.activation(
+                    act[g, t][:, half * BANK : (half + 1) * BANK], accs[half][:], SILU, bias=b_t[:, g, t : t + 1]
+                )
+
+        def new_bank(name):
+            return psum.tile([P, BANK], F32, name=name, tag="bank")
+
+        accs = {(t, half): new_bank("a0%d%d" % (t, half)) for t in range(PACK) for half in range(2)}
+        for a in (VIAL, DILUENT):
+            for t in range(PACK):
+                for half in range(2):
+                    first_stage_pass(accs[t, half], a, 0, t, half)
+        quantise_wd(0, 0, nc.vector.tensor_copy)
+        quantise_wd(0, 1, nc.scalar.copy)
+        wl_t.append(deal_wl(1))
+        for t in range(PACK):
+            finish_tile(0, t, [accs[t, 0], accs[t, 1]])
+        quantise_wd(1, 0, nc.scalar.copy)
+        quantise_wd(1, 1, nc.scalar.copy)
+        for t in range(PACK):
+            pair = [new_bank("a1%d%d" % (t, half)) for half in range(2)]
+            for half in range(2):
+                for a in (VIAL, DILUENT):
+                    first_stage_pass(pair[half], a, 1, t, half)
+            finish_tile(1, t, pair)
+
+        def pick(name, g, t, picked, positions):
+            nc.vector.tensor_tensor(picked[:, t, :], act[g, t][:].indirect(positions[:]), factor[name, g, t][:], ALU.mult)
+
+        def quantise(rounded, width, name):
+            codes = held([P, width], U32, name + "_codes")
+            scales = held([P, width], U8, name + "_sc")
+            step = width if width == BANK else width // 2
+            for c0 in range(0, width, step):
+                nc.vector.quantize_mx(
+                    codes[:, c0 : c0 + step].bitcast(FP8X4), scales[:, c0 : c0 + step],
+                    rounded[:, PACK * c0 : PACK * (c0 + step)],
+                )
+            return codes, scales
+
+        def round_xa(g, picked):
+            rounded = shared([P, PACK * PICKS], BF16, "rounded", 3, "xa_bf%d" % g)
+            nc.scalar.copy(out=woven(rounded), in_=by_rows(picked))
+            return rounded
+
+        def round_xb(g, picked):
+            rounded = shared([P, PACK * PICKS], BF16, "rounded", 3, "xb_bf%d" % g)
+            nc.vector.tensor_tensor(woven(rounded), by_rows(picked), by_rows(level_t[g]), ALU.max)
+            return rounded
+
+        def round_wm(g):
+            rounded = shared([P, PACK * N], BF16, "rounded", 3, "wm_bf%d" % g)
+            nc.scalar.copy(out=woven(rounded), in_=by_rows(wm_raw[g]))
+            return rounded
+
+        xa, xb, wm_q = [], [], []
+        picked_a = shared([P, PACK, PICKS], F32, "picked", 3, "picked_a0")
+        picked_b = shared([P, PACK, PICKS], F32, "picked", 3, "picked_b0")
+        for t in range(PACK):
+            pick("a", 0, t, picked_a, pos1_t)
+            pick("b", 0, t, picked_b, pos2_t)
+        xa_bf = round_xa(0, picked_a)
+        xb_bf = round_xb(0, picked_b)
+        xa.append(quantise(xa_bf, PICKS, "xa0"))
+        xb.append(quantise(xb_bf, PICKS, "xb0"))
+        wm_q.append(quantise(round_wm(0), N, "wm0"))
+        picked_a = shared([P, PACK, PICKS], F32, "picked", 3, "picked_a1")
+        picked_b = shared([P, PACK, PICKS], F32, "picked", 3, "picked_b1")
+        for t in range(PACK):
+            pick("a", 1, t, picked_a, pos1_t)
+        wm_q.append(quantise(round_wm(1), N, "wm1"))
+        xa_bf = round_xa(1, picked_a)
+        for t in range(PACK):
+            pick("b", 1, t, picked_b, pos2_t)
+        xa.append(quantise(xa_bf, PICKS, "xa1"))
+        xb.append(quantise(round_xb(1, picked_b), PICKS, "xb1"))
+
+        ya = shared([P, OUT_TILES, PICKS], F32, "big", 3, "ya")
+        for u in range(OUT_TILES):
+            acc = new_bank("ya%d" % u)
+            for g in range(GROUPS):
+                nc.tensor.matmul_mx(
+                    out=acc[:],
+                    lhsT=wx_t[:, g, 2 * u * P : 2 * (u + 1) * P].bitcast(FP4X4),
+                    lhsT_scale=wx_sc[:, g, u * P : (u + 1) * P],
+                    rhs=xa[g][0][:].bitcast(FP8X4), rhs_scale=xa[g][1][:],
+                    start=(g == 0), stop=(g == GROUPS - 1),
+                )
+            nc.scalar.copy(out=ya[:, u, :], in_=acc[:])
+        for u in range(OUT_TILES):
+            acc = new_bank("yb%d" % u)
+            for g in range(GROUPS):
+                nc.tensor.matmul_mx(
+                    out=acc[:],
+                    lhsT=wm_q[g][0][:, u * P : (u + 1) * P].bitcast(FP8X4),
+                    lhsT_scale=wm_q[g][1][:, u * P : (u + 1) * P],
+                    rhs=xb[g][0][:].bitcast(FP8X4), rhs_scale=xb[g][1][:],
+                    start=(g == 0), stop=(g == GROUPS - 1),
+                )
+            nc.vector.scalar_tensor_tensor(ya[:, u, :], acc[:], b2_t[:, u : u + 1], ya[:, u, :], ALU.add, ALU.max)
+            nc.sync.dma_start(out=out[u * P : (u + 1) * P, :], in_=ya[:, u, :])

@@ -51,16 +51,16 @@ def tile_list_compounding_release_features_kernel(
 
         wv_sc_raw = held([P, H], U8, "wv_sc_raw")
         wl_sc_raw = held([P, H], U8, "wl_sc_raw")
-        tab_sc = held([P, T], U8, "tab_sc")
+        tab_sc = shared([P, T], U8, "tab_sc", 1, "tab_sc")
         wx_sc = held([P, GROUPS, N], U8, "wx_sc")
-        nc.vector.memset(tab_sc[:].bitcast(I32), 0)
         nc.vector.memset(wv_sc_raw[:].bitcast(I32), 0)
+        nc.vector.memset(tab_sc[:].bitcast(I32), 0)
         nc.vector.memset(wl_sc_raw[:].bitcast(I32), 0)
         nc.vector.memset(wx_sc[:].bitcast(I32), 0)
 
         def load_channel_vector(vec, name):
             tile = held([P, GROUPS, 2 * PACK], F32, name)
-            nc.gpsimd.dma_start(out=tile[:, :, 0:PACK], in_=vec.rearrange("(g p t) -> p g t", g=GROUPS, t=PACK))
+            nc.sync.dma_start(out=tile[:, :, 0:PACK], in_=vec.rearrange("(g p t) -> p g t", g=GROUPS, t=PACK))
             return tile
 
         def load_list(src, name):
@@ -68,9 +68,8 @@ def tile_list_compounding_release_features_kernel(
             nc.sync.dma_start(tile[:], src)
             return tile
 
-        def load_table_half(a, half):
+        def load_table(a, cols):
             words = tab_words[a].rearrange("p t i -> p (t i)").bitcast(I32)
-            cols = slice(half * T // 2, (half + 1) * T // 2)
             nc.sync.dma_start(out=table[a][:, cols].bitcast(I32), in_=words[:, cols])
 
         def load_scale_rows(plane, scales, q):
@@ -79,11 +78,11 @@ def tile_list_compounding_release_features_kernel(
             )
 
         def load_table_scales(q):
-            nc.sync.dma_start(
+            nc.gpsimd.dma_start(
                 out=tab_sc[32 * q : 32 * q + 8, :].bitcast(I32),
                 in_=tab_scales[VIAL : DILUENT + 1, 4 * q : 4 * q + 4, :].bitcast(I32),
             )
-            nc.sync.dma_start(
+            nc.gpsimd.dma_start(
                 out=tab_sc[32 * q + 8 : 32 * q + 12, :].bitcast(I32),
                 in_=tab_scales[DRUG, 4 * q : 4 * q + 4, :].bitcast(I32),
             )
@@ -99,40 +98,36 @@ def tile_list_compounding_release_features_kernel(
             nc.sync.dma_start(out=tile[:], in_=wd.rearrange("(p j) c -> p j c", j=PACK)[:, :, g * BANK : (g + 1) * BANK])
             return tile
 
-        def load_rows(src, g, tag, name):
-            tile = shared([P, PACK, src.shape[1]], F32, tag, 3, name)
+        def load_rows(src, g, tag, bufs, name):
+            tile = shared([P, PACK, src.shape[1]], F32, tag, bufs, name)
             rows = src[g * P * PACK : (g + 1) * P * PACK, :]
             nc.sync.dma_start(out=tile[:], in_=rows.rearrange("(p t) c -> p t c", t=PACK))
             return tile
 
-        table = {a: shared([P, T], U32, "big", 3, "table%d" % a) for a in (VIAL, DILUENT, DRUG)}
+        table = {a: shared([P, T], U32, "big%d" % a, 1, "table%d" % a) for a in (VIAL, DILUENT, DRUG)}
+        for q in range(4):
+            load_table_scales(q)
+        offs_t = load_list(offs, "offs_t")
+        load_table(VIAL, slice(0, T // 2))
         gain_t = load_channel_vector(gain, "gain_t")
         dose_t = load_channel_vector(dose, "dose_t")
-        b_t = load_channel_vector(b, "b_t")
-        offs_t = load_list(offs, "offs_t")
-        load_table_half(VIAL, 0)
-        for q in range(3):
-            load_table_scales(q)
-        load_table_half(VIAL, 1)
+        for q in range(4):
+            load_scale_rows(wv_sc_raw, wv_scales, q)
+        load_table(VIAL, slice(T // 2, T))
         wv_raw = held([P, 2 * H], U8, "wv_raw")
         nc.sync.dma_start(out=wv_raw[:].bitcast(I32), in_=wv_words[0].bitcast(I32))
-        load_table_scales(3)
-        for q in range(3):
-            load_scale_rows(wv_sc_raw, wv_scales, q)
-        load_table_half(DILUENT, 0)
-        load_scale_rows(wv_sc_raw, wv_scales, 3)
         wl_raw = [load_wl(0)]
+        load_table(DILUENT, slice(0, T))
         for q in range(4):
             load_scale_rows(wl_sc_raw, wl_scales, q)
-        load_table_half(DILUENT, 1)
+        b_t = load_channel_vector(b, "b_t")
+        load_table(DRUG, slice(0, T))
         pos1_t = load_list(pos1, "pos1_t")
         pos2_t = load_list(pos2, "pos2_t")
-        load_table_half(DRUG, 0)
-        load_table_half(DRUG, 1)
         wd_raw = [load_wd(0), load_wd(1)]
         wl_raw.append(load_wl(1))
-        level_t = [load_rows(level, 0, "mid", "level0")]
-        wm_raw = [load_rows(wm, 0, "big", "wm_raw0")]
+        level_t = [load_rows(level, 0, "mid", 3, "level0")]
+        wm_raw = [load_rows(wm, 0, "big%d" % VIAL, 1, "wm_raw0")]
         wx_t = held([P, GROUPS, 2 * N], U8, "wx_t")
         nc.sync.dma_start(out=wx_t[:].bitcast(I32), in_=wx_words.rearrange("a p c -> p a c").bitcast(I32))
         for q in range(4):
@@ -140,8 +135,8 @@ def tile_list_compounding_release_features_kernel(
                 out=wx_sc[32 * q : 32 * q + 4, :, :].bitcast(I32),
                 in_=wx_scales[:, 4 * q : 4 * q + 4, :].rearrange("a r c -> r a c").bitcast(I32),
             )
-        wm_raw.append(load_rows(wm, 1, "big", "wm_raw1"))
-        level_t.append(load_rows(level, 1, "mid", "level1"))
+        wm_raw.append(load_rows(wm, 1, "big%d" % DRUG, 1, "wm_raw1"))
+        level_t.append(load_rows(level, 1, "mid", 3, "level1"))
         b2_t = held([P, OUT_TILES], F32, "b2_t")
         with nc.allow_non_contiguous_dma(reason="one bias value for each partition"):
             nc.sync.dma_start(out=b2_t[:], in_=b2.rearrange("(u p) -> p u", p=P))
@@ -150,11 +145,11 @@ def tile_list_compounding_release_features_kernel(
         nc.vector.tensor_tensor(gain_dose[:], gain_t[:, :, 0:PACK], dose_t[:, :, 0:PACK], ALU.mult)
         factor = {}
         for g in range(GROUPS):
-            for t in range(PACK):
-                for name, vec in (("a", gain_dose), ("b", gain_t)):
-                    tile = held([P, PICKS], F32, "factor_%s%d%d" % (name, g, t))
-                    nc.scalar.copy(out=tile[:], in_=vec[:, g, t : t + 1].to_broadcast([P, PICKS]))
-                    factor[name, g, t] = tile
+            for name, vec in (("a", gain_dose), ("b", gain_t)):
+                tile = shared([P, PACK, PICKS], F32, "factor_%s%d" % (name, g), 1, "factor_%s%d" % (name, g))
+                for t in range(PACK):
+                    nc.scalar.copy(out=tile[:, t, :], in_=vec[:, g, t : t + 1].to_broadcast([P, PICKS]))
+                factor[name, g] = tile
 
         def deal_scales(raw, name):
             tile = held([P, H], U8, name)
@@ -169,13 +164,13 @@ def tile_list_compounding_release_features_kernel(
             nc.vector.tensor_copy(out=tile[:], in_=wl_raw[g][:].rearrange("p (m t) -> p t m", t=PACK))
             return tile
 
-        def gather_table(a):
-            tile = held([P, S], U32, "v%d" % a)
+        def gather_table(a, tag):
+            tile = shared([P, S], U32, tag, 1, "v%d" % a)
             nc.vector.tensor_copy(tile[:], table[a][:].indirect(offs_t[:]))
             return tile
 
         v = {}
-        v[VIAL] = gather_table(VIAL)
+        v[VIAL] = gather_table(VIAL, "v_vial")
         wv_sc = deal_scales(wv_sc_raw, "wv_sc")
         wv_t = held([P, 2 * H], U8, "wv_t")
         nc.vector.tensor_copy(
@@ -184,10 +179,10 @@ def tile_list_compounding_release_features_kernel(
         )
         v_sc = held([P, S], U8, "v_sc")
         nc.vector.tensor_copy(v_sc[:], tab_sc[:].indirect(offs_t[:]))
-        v[DILUENT] = gather_table(DILUENT)
+        v[DILUENT] = gather_table(DILUENT, "tab_sc")
         wl_sc = deal_scales(wl_sc_raw, "wl_sc")
         wl_t = [deal_wl(0)]
-        v[DRUG] = gather_table(DRUG)
+        v[DRUG] = gather_table(DRUG, "big%d" % DILUENT)
 
         wd_codes, wd_sc = {}, {}
 
@@ -255,7 +250,7 @@ def tile_list_compounding_release_features_kernel(
             finish_tile(1, t, pair)
 
         def pick(name, g, t, picked, positions):
-            nc.vector.tensor_tensor(picked[:, t, :], act[g, t][:].indirect(positions[:]), factor[name, g, t][:], ALU.mult)
+            nc.vector.tensor_tensor(picked[:, t, :], act[g, t][:].indirect(positions[:]), factor[name, g][:, t, :], ALU.mult)
 
         def quantise(rounded, width, name):
             codes = held([P, width], U32, name + "_codes")
@@ -269,23 +264,23 @@ def tile_list_compounding_release_features_kernel(
             return codes, scales
 
         def round_xa(g, picked):
-            rounded = shared([P, PACK * PICKS], BF16, "rounded", 3, "xa_bf%d" % g)
+            rounded = shared([P, PACK * PICKS], BF16, "xa_bf%d" % g, 1, "xa_bf%d" % g)
             nc.scalar.copy(out=woven(rounded), in_=by_rows(picked))
             return rounded
 
         def round_xb(g, picked):
-            rounded = shared([P, PACK * PICKS], BF16, "rounded", 3, "xb_bf%d" % g)
+            rounded = shared([P, PACK * PICKS], BF16, ("xb_bf0", "xa_bf1")[g], 1, "xb_bf%d" % g)
             nc.vector.tensor_tensor(woven(rounded), by_rows(picked), by_rows(level_t[g]), ALU.max)
             return rounded
 
         def round_wm(g):
-            rounded = shared([P, PACK * N], BF16, "rounded", 3, "wm_bf%d" % g)
+            rounded = shared([P, PACK * N], BF16, "wm_bf%d" % g, 1, "wm_bf%d" % g)
             nc.scalar.copy(out=woven(rounded), in_=by_rows(wm_raw[g]))
             return rounded
 
         xa, xb, wm_q = [], [], []
-        picked_a = shared([P, PACK, PICKS], F32, "picked", 3, "picked_a0")
-        picked_b = shared([P, PACK, PICKS], F32, "picked", 3, "picked_b0")
+        picked_a = shared([P, PACK, PICKS], F32, "picked_a0", 1, "picked_a0")
+        picked_b = shared([P, PACK, PICKS], F32, "picked_b0", 1, "picked_b0")
         for t in range(PACK):
             pick("a", 0, t, picked_a, pos1_t)
             pick("b", 0, t, picked_b, pos2_t)
@@ -294,8 +289,8 @@ def tile_list_compounding_release_features_kernel(
         xa.append(quantise(xa_bf, PICKS, "xa0"))
         xb.append(quantise(xb_bf, PICKS, "xb0"))
         wm_q.append(quantise(round_wm(0), N, "wm0"))
-        picked_a = shared([P, PACK, PICKS], F32, "picked", 3, "picked_a1")
-        picked_b = shared([P, PACK, PICKS], F32, "picked", 3, "picked_b1")
+        picked_a = shared([P, PACK, PICKS], F32, "picked_b0", 1, "picked_a1")
+        picked_b = shared([P, PACK, PICKS], F32, "factor_a1", 1, "picked_b1")
         for t in range(PACK):
             pick("a", 1, t, picked_a, pos1_t)
         wm_q.append(quantise(round_wm(1), N, "wm1"))
@@ -305,7 +300,7 @@ def tile_list_compounding_release_features_kernel(
         xa.append(quantise(xa_bf, PICKS, "xa1"))
         xb.append(quantise(round_xb(1, picked_b), PICKS, "xb1"))
 
-        ya = shared([P, OUT_TILES, PICKS], F32, "big", 3, "ya")
+        ya = shared([P, OUT_TILES, PICKS], F32, "big%d" % VIAL, 1, "ya")
         for u in range(OUT_TILES):
             acc = new_bank("ya%d" % u)
             for g in range(GROUPS):

@@ -49,13 +49,11 @@ def tile_list_compounding_release_features_kernel(
         def by_rows(tile):
             return tile[:].rearrange("p t (c i) -> p c t i", i=RUN)
 
-        wv_sc_raw = held([P, H], U8, "wv_sc_raw")
-        wl_sc_raw = held([P, H], U8, "wl_sc_raw")
-        tab_sc = shared([P, T], U8, "tab_sc", 1, "tab_sc")
+        w_sc_raw = held([P, H], U8, "w_sc_raw")
+        tab_sc = held([P, T], U8, "tab_sc")
         wx_sc = held([P, GROUPS, N], U8, "wx_sc")
-        nc.vector.memset(wv_sc_raw[:].bitcast(I32), 0)
         nc.vector.memset(tab_sc[:].bitcast(I32), 0)
-        nc.vector.memset(wl_sc_raw[:].bitcast(I32), 0)
+        nc.vector.memset(w_sc_raw[:].bitcast(I32), 0)
         nc.vector.memset(wx_sc[:].bitcast(I32), 0)
 
         def load_channel_vector(vec, name):
@@ -72,17 +70,19 @@ def tile_list_compounding_release_features_kernel(
             words = tab_words[a].rearrange("p t i -> p (t i)").bitcast(I32)
             nc.sync.dma_start(out=table[a][:, cols].bitcast(I32), in_=words[:, cols])
 
-        def load_scale_rows(plane, scales, q):
-            nc.sync.dma_start(
-                out=plane[32 * q : 32 * q + 4, :].bitcast(I32), in_=scales[0, 4 * q : 4 * q + 4, :].bitcast(I32)
-            )
+        def load_weight_scales(scales, a):
+            for q in range(4):
+                row = 32 * q + PLANE_ROW[a]
+                nc.sync.dma_start(
+                    out=w_sc_raw[row : row + 4, :].bitcast(I32), in_=scales[0, 4 * q : 4 * q + 4, :].bitcast(I32)
+                )
 
         def load_table_scales(q):
-            nc.gpsimd.dma_start(
+            nc.sync.dma_start(
                 out=tab_sc[32 * q : 32 * q + 8, :].bitcast(I32),
                 in_=tab_scales[VIAL : DILUENT + 1, 4 * q : 4 * q + 4, :].bitcast(I32),
             )
-            nc.gpsimd.dma_start(
+            nc.sync.dma_start(
                 out=tab_sc[32 * q + 8 : 32 * q + 12, :].bitcast(I32),
                 in_=tab_scales[DRUG, 4 * q : 4 * q + 4, :].bitcast(I32),
             )
@@ -98,36 +98,36 @@ def tile_list_compounding_release_features_kernel(
             nc.sync.dma_start(out=tile[:], in_=wd.rearrange("(p j) c -> p j c", j=PACK)[:, :, g * BANK : (g + 1) * BANK])
             return tile
 
-        def load_rows(src, g, tag, bufs, name):
-            tile = shared([P, PACK, src.shape[1]], F32, tag, bufs, name)
+        def load_rows(src, g, tile):
             rows = src[g * P * PACK : (g + 1) * P * PACK, :]
             nc.sync.dma_start(out=tile[:], in_=rows.rearrange("(p t) c -> p t c", t=PACK))
             return tile
 
         table = {a: shared([P, T], U32, "big%d" % a, 1, "table%d" % a) for a in (VIAL, DILUENT, DRUG)}
-        for q in range(4):
-            load_table_scales(q)
         offs_t = load_list(offs, "offs_t")
         load_table(VIAL, slice(0, T // 2))
-        gain_t = load_channel_vector(gain, "gain_t")
-        dose_t = load_channel_vector(dose, "dose_t")
-        for q in range(4):
-            load_scale_rows(wv_sc_raw, wv_scales, q)
+        for q in range(3):
+            load_table_scales(q)
         load_table(VIAL, slice(T // 2, T))
+        load_table_scales(3)
+        load_weight_scales(wv_scales, VIAL)
+        load_table(DILUENT, slice(0, T // 2))
+        load_weight_scales(wl_scales, DILUENT)
         wv_raw = held([P, 2 * H], U8, "wv_raw")
         nc.sync.dma_start(out=wv_raw[:].bitcast(I32), in_=wv_words[0].bitcast(I32))
+        gain_t = load_channel_vector(gain, "gain_t")
+        load_table(DILUENT, slice(T // 2, T))
+        dose_t = load_channel_vector(dose, "dose_t")
         wl_raw = [load_wl(0)]
-        load_table(DILUENT, slice(0, T))
-        for q in range(4):
-            load_scale_rows(wl_sc_raw, wl_scales, q)
         b_t = load_channel_vector(b, "b_t")
-        load_table(DRUG, slice(0, T))
         pos1_t = load_list(pos1, "pos1_t")
         pos2_t = load_list(pos2, "pos2_t")
-        wd_raw = [load_wd(0), load_wd(1)]
+        load_table(DRUG, slice(0, T))
+        wd_raw = [load_wd(0)]
         wl_raw.append(load_wl(1))
-        level_t = [load_rows(level, 0, "mid", 3, "level0")]
-        wm_raw = [load_rows(wm, 0, "big%d" % VIAL, 1, "wm_raw0")]
+        wd_raw.append(load_wd(1))
+        level_t = [load_rows(level, 0, shared([P, PACK, PICKS], F32, "mid", 3, "level0"))]
+        wm_raw = [load_rows(wm, 0, shared([P, PACK, N], F32, "big%d" % VIAL, 1, "wm_raw0"))]
         wx_t = held([P, GROUPS, 2 * N], U8, "wx_t")
         nc.sync.dma_start(out=wx_t[:].bitcast(I32), in_=wx_words.rearrange("a p c -> p a c").bitcast(I32))
         for q in range(4):
@@ -135,59 +135,53 @@ def tile_list_compounding_release_features_kernel(
                 out=wx_sc[32 * q : 32 * q + 4, :, :].bitcast(I32),
                 in_=wx_scales[:, 4 * q : 4 * q + 4, :].rearrange("a r c -> r a c").bitcast(I32),
             )
-        wm_raw.append(load_rows(wm, 1, "big%d" % DRUG, 1, "wm_raw1"))
-        level_t.append(load_rows(level, 1, "mid", 3, "level1"))
+        wm_raw.append(load_rows(wm, 1, shared([P, PACK, N], F32, "big%d" % DRUG, 1, "wm_raw1")))
+        level_t.append(load_rows(level, 1, shared([P, PACK, PICKS], F32, "mid", 3, "level1")))
         b2_t = held([P, OUT_TILES], F32, "b2_t")
         with nc.allow_non_contiguous_dma(reason="one bias value for each partition"):
             nc.sync.dma_start(out=b2_t[:], in_=b2.rearrange("(u p) -> p u", p=P))
 
         gain_dose = held([P, GROUPS, PACK], F32, "gain_dose")
         nc.vector.tensor_tensor(gain_dose[:], gain_t[:, :, 0:PACK], dose_t[:, :, 0:PACK], ALU.mult)
-        factor = {}
-        for g in range(GROUPS):
-            for name, vec in (("a", gain_dose), ("b", gain_t)):
-                tile = shared([P, PACK, PICKS], F32, "factor_%s%d" % (name, g), 1, "factor_%s%d" % (name, g))
-                for t in range(PACK):
-                    nc.scalar.copy(out=tile[:, t, :], in_=vec[:, g, t : t + 1].to_broadcast([P, PICKS]))
-                factor[name, g] = tile
 
-        def deal_scales(raw, name):
-            tile = held([P, H], U8, name)
-            nc.vector.tensor_copy(
-                out=tile[:].rearrange("p (g t m) -> p g t m", g=GROUPS, t=PACK),
-                in_=raw[:].rearrange("p (g m t) -> p g t m", g=GROUPS, t=PACK),
-            )
-            return tile
+        factor = []
+        for g in range(GROUPS):
+            factor.append(shared([P, PACK, PICKS], F32, "factor%d" % g, 1, "factor%d" % g))
+            for t in range(PACK):
+                nc.scalar.copy(out=factor[g][:, t, :], in_=gain_dose[:, g, t : t + 1].to_broadcast([P, PICKS]))
 
         def deal_wl(g):
             tile = held([P, PACK, P], I32, "wl_t%d" % g)
             nc.vector.tensor_copy(out=tile[:], in_=wl_raw[g][:].rearrange("p (m t) -> p t m", t=PACK))
             return tile
 
-        def gather_table(a, tag):
-            tile = shared([P, S], U32, tag, 1, "v%d" % a)
+        def gather_table(a):
+            tile = held([P, S], U32, "v%d" % a)
             nc.vector.tensor_copy(tile[:], table[a][:].indirect(offs_t[:]))
             return tile
 
         v = {}
-        v[VIAL] = gather_table(VIAL, "v_vial")
-        wv_sc = deal_scales(wv_sc_raw, "wv_sc")
-        wv_t = held([P, 2 * H], U8, "wv_t")
-        nc.vector.tensor_copy(
-            out=wv_t[:].rearrange("p (g t m e) -> p g t m e", g=GROUPS, t=PACK, e=2),
-            in_=wv_raw[:].rearrange("p (g m t e) -> p g t m e", g=GROUPS, t=PACK, e=2),
-        )
+        v[VIAL] = gather_table(VIAL)
         v_sc = held([P, S], U8, "v_sc")
         nc.vector.tensor_copy(v_sc[:], tab_sc[:].indirect(offs_t[:]))
-        v[DILUENT] = gather_table(DILUENT, "tab_sc")
-        wl_sc = deal_scales(wl_sc_raw, "wl_sc")
+        w_sc = held([P, H], U8, "w_sc")
+        nc.vector.tensor_copy(
+            out=w_sc[:].rearrange("p (g t m) -> p g t m", g=GROUPS, t=PACK),
+            in_=w_sc_raw[:].rearrange("p (g m t) -> p g t m", g=GROUPS, t=PACK),
+        )
+        wv_t = held([P, 2 * H], U8, "wv_t")
+        nc.vector.tensor_copy(
+            out=wv_t[:].bitcast(U16).rearrange("p (g t m) -> p g t m", g=GROUPS, t=PACK),
+            in_=wv_raw[:].bitcast(U16).rearrange("p (g m t) -> p g t m", g=GROUPS, t=PACK),
+        )
+        v[DILUENT] = gather_table(DILUENT)
         wl_t = [deal_wl(0)]
-        v[DRUG] = gather_table(DRUG, "big%d" % DILUENT)
+        v[DRUG] = gather_table(DRUG)
 
         wd_codes, wd_sc = {}, {}
 
         def quantise_wd(g, u, cast):
-            rounded = shared([P, 2, P, PACK], BF16, "wd_bf", 2, "wd_bf%d%d" % (g, u))
+            rounded = held([P, 2, P, PACK], BF16, "wd_bf%d%d" % (g, u))
             cast(
                 out=rounded[:].rearrange("p e m j -> p m j e"),
                 in_=wd_raw[g][:].rearrange("p j (m u e) -> p u m j e", u=2, e=2)[:, u],
@@ -204,10 +198,10 @@ def tile_list_compounding_release_features_kernel(
             col0 = (g * PACK + t) * P
             if a == VIAL:
                 lhsT = wv_t[:, 2 * col0 : 2 * (col0 + P)].bitcast(FP4X4)
-                lhsT_scale = wv_sc[:, col0 : col0 + P]
+                lhsT_scale = w_sc[PLANE_ROW[a] : P, col0 : col0 + P]
             elif a == DILUENT:
                 lhsT = wl_t[g][:, t, :].bitcast(FP8X4)
-                lhsT_scale = wl_sc[:, col0 : col0 + P]
+                lhsT_scale = w_sc[PLANE_ROW[a] : P, col0 : col0 + P]
             else:
                 lhsT = wd_codes[g, t].bitcast(FP8X4)
                 lhsT_scale = wd_sc[g, t]
@@ -236,7 +230,7 @@ def tile_list_compounding_release_features_kernel(
                 for half in range(2):
                     first_stage_pass(accs[t, half], a, 0, t, half)
         quantise_wd(0, 0, nc.vector.tensor_copy)
-        quantise_wd(0, 1, nc.scalar.copy)
+        quantise_wd(0, 1, nc.vector.tensor_copy)
         wl_t.append(deal_wl(1))
         for t in range(PACK):
             finish_tile(0, t, [accs[t, 0], accs[t, 1]])
@@ -249,8 +243,15 @@ def tile_list_compounding_release_features_kernel(
                     first_stage_pass(pair[half], a, 1, t, half)
             finish_tile(1, t, pair)
 
-        def pick(name, g, t, picked, positions):
-            nc.vector.tensor_tensor(picked[:, t, :], act[g, t][:].indirect(positions[:]), factor[name, g][:, t, :], ALU.mult)
+        picked_a = [held([P, PACK, PICKS], F32, "picked_a%d" % g) for g in range(GROUPS)]
+
+        def pick_a(g, t):
+            nc.vector.tensor_tensor(picked_a[g][:, t, :], act[g, t][:].indirect(pos1_t[:]), factor[g][:, t, :], ALU.mult)
+
+        def pick_b(g, t, tag):
+            picked = shared([P, PICKS], F32, tag, 1, "picked_b%d%d" % (g, t))
+            nc.vector.tensor_copy(picked[:], act[g, t][:].indirect(pos2_t[:]))
+            return picked
 
         def quantise(rounded, width, name):
             codes = held([P, width], U32, name + "_codes")
@@ -263,42 +264,45 @@ def tile_list_compounding_release_features_kernel(
                 )
             return codes, scales
 
-        def round_xa(g, picked):
-            rounded = shared([P, PACK * PICKS], BF16, "xa_bf%d" % g, 1, "xa_bf%d" % g)
-            nc.scalar.copy(out=woven(rounded), in_=by_rows(picked))
+        def weave(rows, copy, tag, name):
+            rounded = shared([P, PACK * rows.shape[2]], BF16, tag, 1, name)
+            copy(out=woven(rounded), in_=by_rows(rows))
             return rounded
 
-        def round_xb(g, picked):
-            rounded = shared([P, PACK * PICKS], BF16, ("xb_bf0", "xa_bf1")[g], 1, "xb_bf%d" % g)
-            nc.vector.tensor_tensor(woven(rounded), by_rows(picked), by_rows(level_t[g]), ALU.max)
-            return rounded
+        def round_xb(rows, g, t, picked):
+            nc.vector.scalar_tensor_tensor(
+                rows[:, t, :], picked[:], gain_t[:, g, t : t + 1], level_t[g][:, t, :], ALU.mult, ALU.max
+            )
 
-        def round_wm(g):
-            rounded = shared([P, PACK * N], BF16, "wm_bf%d" % g, 1, "wm_bf%d" % g)
-            nc.scalar.copy(out=woven(rounded), in_=by_rows(wm_raw[g]))
-            return rounded
+        xb_rows = held([P, PACK, PICKS], BF16, "xb_rows0")
+        for t in range(PACK):
+            picked = pick_b(0, t, "picked_b%d" % (t % 2))
+            pick_a(0, t)
+            round_xb(xb_rows, 0, t, picked)
+        for t in range(PACK):
+            pick_a(1, t)
+        wm_bf = [weave(wm_raw[0], nc.scalar.copy, "wm_bf0", "wm_bf0")]
+        xb_bf0 = weave(xb_rows, nc.scalar.copy, "xb_bf0", "xb_bf0")
+        xa_bf0 = weave(picked_a[0], nc.scalar.copy, "xa_bf0", "xa_bf0")
+        xa_bf1 = weave(picked_a[1], nc.scalar.copy, "xa_bf1", "xa_bf1")
+        wm_bf.append(weave(wm_raw[1], nc.scalar.copy, "wm_bf1", "wm_bf1"))
 
-        xa, xb, wm_q = [], [], []
-        picked_a = shared([P, PACK, PICKS], F32, "picked_a0", 1, "picked_a0")
-        picked_b = shared([P, PACK, PICKS], F32, "picked_b0", 1, "picked_b0")
-        for t in range(PACK):
-            pick("a", 0, t, picked_a, pos1_t)
-            pick("b", 0, t, picked_b, pos2_t)
-        xa_bf = round_xa(0, picked_a)
-        xb_bf = round_xb(0, picked_b)
-        xa.append(quantise(xa_bf, PICKS, "xa0"))
-        xb.append(quantise(xb_bf, PICKS, "xb0"))
-        wm_q.append(quantise(round_wm(0), N, "wm0"))
-        picked_a = shared([P, PACK, PICKS], F32, "picked_b0", 1, "picked_a1")
-        picked_b = shared([P, PACK, PICKS], F32, "factor_a1", 1, "picked_b1")
-        for t in range(PACK):
-            pick("a", 1, t, picked_a, pos1_t)
-        wm_q.append(quantise(round_wm(1), N, "wm1"))
-        xa_bf = round_xa(1, picked_a)
-        for t in range(PACK):
-            pick("b", 1, t, picked_b, pos2_t)
-        xa.append(quantise(xa_bf, PICKS, "xa1"))
-        xb.append(quantise(round_xb(1, picked_b), PICKS, "xb1"))
+        picked = [pick_b(1, 0, "factor1")]
+        xb = [quantise(xb_bf0, PICKS, "xb0")]
+        xa = [quantise(xa_bf0, PICKS, "xa0")]
+        picked.append(pick_b(1, 1, "xa_bf0"))
+        xb_rows = shared([P, PACK, PICKS], BF16, "xb_bf0", 1, "xb_rows1")
+        round_xb(xb_rows, 1, 0, picked[0])
+        xa.append(quantise(xa_bf1, PICKS, "xa1"))
+        round_xb(xb_rows, 1, 1, picked[1])
+        picked.append(pick_b(1, 2, "xa_bf1"))
+        wm_q = [quantise(wm_bf[0], N, "wm0")]
+        picked.append(pick_b(1, 3, "wm_bf0"))
+        round_xb(xb_rows, 1, 2, picked[2])
+        round_xb(xb_rows, 1, 3, picked[3])
+        xb_bf1 = weave(xb_rows, nc.vector.tensor_copy, "xb_bf1", "xb_bf1")
+        wm_q.append(quantise(wm_bf[1], N, "wm1"))
+        xb.append(quantise(xb_bf1, PICKS, "xb1"))
 
         ya = shared([P, OUT_TILES, PICKS], F32, "big%d" % VIAL, 1, "ya")
         for u in range(OUT_TILES):

from contextlib import ExitStack

import concourse.mybir as mybir

K, KB, H, N, T, S, PICKS = 1536, 512, 1024, 768, 4096, 1024, 512
FLOPS = 2 * K * H * S + 2 * 2 * H * N * PICKS

F32 = mybir.dt.float32
BF16 = mybir.dt.bfloat16
I32 = mybir.dt.int32
U32 = mybir.dt.uint32
U16 = mybir.dt.uint16
U8 = mybir.dt.uint8
FP8X4 = mybir.dt.float8_e4m3fn_x4
FP4X4 = mybir.dt.float4_e2m1fn_x4
ALU = mybir.AluOpType
SILU = mybir.ActivationFunctionType.Silu

P = 128
PACK = 4
BANK = 512
GROUPS = H // (P * PACK)
OUT_TILES = N // P
DRUG, VIAL, DILUENT = 0, 1, 2
PLANE_ROW = {VIAL: 0, DILUENT: 4, DRUG: 8}
RUN = 4


def tile_list_compounding_release_features_kernel(
    tc, tab_words, tab_scales, offs, pos1, pos2, wd, wv_words, wv_scales, wl_words, wl_scales,
    b, gain, dose, level, wx_words, wx_scales, wm, b2, out,
):
    nc = tc.nc

    with ExitStack() as ctx:
        keep = ctx.enter_context(tc.tile_pool(name="keep", bufs=1))
        ring = ctx.enter_context(tc.tile_pool(name="ring", bufs=1))
        psum = ctx.enter_context(tc.psum_pool(name="psum", bufs=8))

        def held(shape, dtype, name):
            return keep.tile(shape, dtype, name=name, align_bytes=64)

        def shared(shape, dtype, tag, bufs, name):
            return ring.tile(shape, dtype, name=name, tag=tag, bufs=bufs, align_bytes=64)

        def woven(tile):
            return tile[:].rearrange("p (c i t) -> p c t i", i=RUN, t=PACK)

        def by_rows(tile):
            return tile[:].rearrange("p t (c i) -> p c t i", i=RUN)

        w_sc_raw = held([P, H], U8, "w_sc_raw")
        tab_sc = held([P, T], U8, "tab_sc")
        wx_sc = held([P, GROUPS, N], U8, "wx_sc")
        nc.vector.memset(tab_sc[:].bitcast(I32), 0)
        nc.vector.memset(w_sc_raw[:].bitcast(I32), 0)
        nc.vector.memset(wx_sc[:].bitcast(I32), 0)

        def load_channel_vector(vec, name):
            tile = held([P, GROUPS, 2 * PACK], F32, name)
            nc.sync.dma_start(out=tile[:, :, 0:PACK], in_=vec.rearrange("(g p t) -> p g t", g=GROUPS, t=PACK))
            return tile

        def load_list(src, name):
            tile = held(list(src.shape), U16, name)
            nc.sync.dma_start(tile[:], src)
            return tile

        def load_table(a, cols):
            words = tab_words[a].rearrange("p t i -> p (t i)").bitcast(I32)
            nc.sync.dma_start(out=table[a][:, cols].bitcast(I32), in_=words[:, cols])

        def load_weight_scales(scales, a):
            for q in range(4):
                row = 32 * q + PLANE_ROW[a]
                nc.sync.dma_start(
                    out=w_sc_raw[row : row + 4, :].bitcast(I32), in_=scales[0, 4 * q : 4 * q + 4, :].bitcast(I32)
                )

        def load_table_scales(q):
            nc.sync.dma_start(
                out=tab_sc[32 * q : 32 * q + 8, :].bitcast(I32),
                in_=tab_scales[VIAL : DILUENT + 1, 4 * q : 4 * q + 4, :].bitcast(I32),
            )
            nc.sync.dma_start(
                out=tab_sc[32 * q + 8 : 32 * q + 12, :].bitcast(I32),
                in_=tab_scales[DRUG, 4 * q : 4 * q + 4, :].bitcast(I32),
            )

        def load_wl(g):
            tile = held([P, BANK], I32, "wl_raw%d" % g)
            words = wl_words[0].rearrange("p c i -> p (c i)")
            nc.sync.dma_start(out=tile[:], in_=words[:, g * BANK * PACK : (g + 1) * BANK * PACK].bitcast(I32))
            return tile

        def load_wd(g):
            tile = shared([P, PACK, BANK], F32, "mid", 3, "wd_raw%d" % g)
            nc.sync.dma_start(out=tile[:], in_=wd.rearrange("(p j) c -> p j c", j=PACK)[:, :, g * BANK : (g + 1) * BANK])
            return tile

        def load_rows(src, g, tile):
            rows = src[g * P * PACK : (g + 1) * P * PACK, :]
            nc.sync.dma_start(out=tile[:], in_=rows.rearrange("(p t) c -> p t c", t=PACK))
            return tile

        table = {a: shared([P, T], U32, "big%d" % a, 1, "table%d" % a) for a in (VIAL, DILUENT, DRUG)}
        offs_t = load_list(offs, "offs_t")
        load_table(VIAL, slice(0, T // 2))
        for q in range(3):
            load_table_scales(q)
        load_table(VIAL, slice(T // 2, T))
        load_table_scales(3)
        load_weight_scales(wv_scales, VIAL)
        load_table(DILUENT, slice(0, T // 2))
        load_weight_scales(wl_scales, DILUENT)
        wv_raw = held([P, 2 * H], U8, "wv_raw")
        nc.sync.dma_start(out=wv_raw[:].bitcast(I32), in_=wv_words[0].bitcast(I32))
        gain_t = load_channel_vector(gain, "gain_t")
        load_table(DILUENT, slice(T // 2, T))
        dose_t = load_channel_vector(dose, "dose_t")
        wl_raw = [load_wl(0)]
        b_t = load_channel_vector(b, "b_t")
        pos1_t = load_list(pos1, "pos1_t")
        pos2_t = load_list(pos2, "pos2_t")
        load_table(DRUG, slice(0, T))
        wd_raw = [load_wd(0)]
        wl_raw.append(load_wl(1))
        wd_raw.append(load_wd(1))
        level_t = [load_rows(level, 0, shared([P, PACK, PICKS], F32, "mid", 3, "level0"))]
        wm_raw = [load_rows(wm, 0, shared([P, PACK, N], F32, "big%d" % VIAL, 1, "wm_raw0"))]
        wx_t = held([P, GROUPS, 2 * N], U8, "wx_t")
        nc.sync.dma_start(out=wx_t[:].bitcast(I32), in_=wx_words.rearrange("a p c -> p a c").bitcast(I32))
        for q in range(4):
            nc.sync.dma_start(
                out=wx_sc[32 * q : 32 * q + 4, :, :].bitcast(I32),
                in_=wx_scales[:, 4 * q : 4 * q + 4, :].rearrange("a r c -> r a c").bitcast(I32),
            )
        wm_raw.append(load_rows(wm, 1, shared([P, PACK, N], F32, "big%d" % DRUG, 1, "wm_raw1")))
        level_t.append(load_rows(level, 1, shared([P, PACK, PICKS], F32, "mid", 3, "level1")))
        b2_t = held([P, OUT_TILES], F32, "b2_t")
        with nc.allow_non_contiguous_dma(reason="one bias value for each partition"):
            nc.sync.dma_start(out=b2_t[:], in_=b2.rearrange("(u p) -> p u", p=P))

        gain_dose = held([P, GROUPS, PACK], F32, "gain_dose")
        nc.vector.tensor_tensor(gain_dose[:], gain_t[:, :, 0:PACK], dose_t[:, :, 0:PACK], ALU.mult)

        factor = []
        for g in range(GROUPS):
            factor.append(shared([P, PACK, PICKS], F32, "factor%d" % g, 1, "factor%d" % g))
            for t in range(PACK):
                nc.scalar.copy(out=factor[g][:, t, :], in_=gain_dose[:, g, t : t + 1].to_broadcast([P, PICKS]))

        def deal_wl(g):
            tile = held([P, PACK, P], I32, "wl_t%d" % g)
            nc.vector.tensor_copy(out=tile[:], in_=wl_raw[g][:].rearrange("p (m t) -> p t m", t=PACK))
            return tile

        def gather_table(a):
            tile = held([P, S], U32, "v%d" % a)
            nc.vector.tensor_copy(tile[:], table[a][:].indirect(offs_t[:]))
            return tile

        v = {}
        v[VIAL] = gather_table(VIAL)
        v_sc = held([P, S], U8, "v_sc")
        nc.vector.tensor_copy(v_sc[:], tab_sc[:].indirect(offs_t[:]))
        w_sc = held([P, H], U8, "w_sc")
        nc.vector.tensor_copy(
            out=w_sc[:].rearrange("p (g t m) -> p g t m", g=GROUPS, t=PACK),
            in_=w_sc_raw[:].rearrange("p (g m t) -> p g t m", g=GROUPS, t=PACK),
        )
        wv_t = held([P, 2 * H], U8, "wv_t")
        nc.vector.tensor_copy(
            out=wv_t[:].bitcast(U16).rearrange("p (g t m) -> p g t m", g=GROUPS, t=PACK),
            in_=wv_raw[:].bitcast(U16).rearrange("p (g m t) -> p g t m", g=GROUPS, t=PACK),
        )
        v[DILUENT] = gather_table(DILUENT)
        wl_t = [deal_wl(0)]
        v[DRUG] = gather_table(DRUG)

        wd_codes, wd_sc = {}, {}

        def quantise_wd(g, u, cast):
            rounded = held([P, 2, P, PACK], BF16, "wd_bf%d%d" % (g, u))
            cast(
                out=rounded[:].rearrange("p e m j -> p m j e"),
                in_=wd_raw[g][:].rearrange("p j (m u e) -> p u m j e", u=2, e=2)[:, u],
            )
            codes = held([P, 2 * P], U32, "wd_codes%d%d" % (g, u))
            scales = held([P, 2 * P], U8, "wd_sc%d%d" % (g, u))
            nc.vector.quantize_mx(codes[:].bitcast(FP8X4), scales[:], rounded[:].rearrange("p e m j -> p (e m j)"))
            for e in range(2):
                wd_codes[g, 2 * u + e] = codes[:, e * P : (e + 1) * P]
                wd_sc[g, 2 * u + e] = scales[:, e * P : (e + 1) * P]

        def first_stage_pass(acc, a, g, t, half):
            cols = slice(half * BANK, (half + 1) * BANK)
            col0 = (g * PACK + t) * P
            if a == VIAL:
                lhsT = wv_t[:, 2 * col0 : 2 * (col0 + P)].bitcast(FP4X4)
                lhsT_scale = w_sc[PLANE_ROW[a] : P, col0 : col0 + P]
            elif a == DILUENT:
                lhsT = wl_t[g][:, t, :].bitcast(FP8X4)
                lhsT_scale = w_sc[PLANE_ROW[a] : P, col0 : col0 + P]
            else:
                lhsT = wd_codes[g, t].bitcast(FP8X4)
                lhsT_scale = wd_sc[g, t]
            nc.tensor.matmul_mx(
                out=acc[:], lhsT=lhsT, lhsT_scale=lhsT_scale,
                rhs=v[a][:, cols].bitcast(FP8X4), rhs_scale=v_sc[PLANE_ROW[a] : P, cols],
                start=(a == VIAL), stop=(a == DRUG),
            )

        act = {}

        def finish_tile(g, t, accs):
            act[g, t] = shared([P, S], F32, "act", 6, "act%d%d" % (g, t))
            for half in range(2):
                first_stage_pass(accs[half], DRUG, g, t, half)
                nc.scalar.activation(
                    act[g, t][:, half * BANK : (half + 1) * BANK], accs[half][:], SILU, bias=b_t[:, g, t : t + 1]
                )

        def new_bank(name):
            return psum.tile([P, BANK], F32, name=name, tag="bank")

        accs = {(t, half): new_bank("a0%d%d" % (t, half)) for t in range(PACK) for half in range(2)}
        for a in (VIAL, DILUENT):
            for t in range(PACK):
                for half in range(2):
                    first_stage_pass(accs[t, half], a, 0, t, half)
        quantise_wd(0, 0, nc.vector.tensor_copy)
        quantise_wd(0, 1, nc.vector.tensor_copy)
        wl_t.append(deal_wl(1))
        for t in range(PACK):
            finish_tile(0, t, [accs[t, 0], accs[t, 1]])
        quantise_wd(1, 0, nc.scalar.copy)
        quantise_wd(1, 1, nc.scalar.copy)
        for t in range(PACK):
            pair = [new_bank("a1%d%d" % (t, half)) for half in range(2)]
            for half in range(2):
                for a in (VIAL, DILUENT):
                    first_stage_pass(pair[half], a, 1, t, half)
            finish_tile(1, t, pair)

        picked_a = [held([P, PACK, PICKS], F32, "picked_a%d" % g) for g in range(GROUPS)]

        def pick_a(g, t):
            nc.vector.tensor_tensor(picked_a[g][:, t, :], act[g, t][:].indirect(pos1_t[:]), factor[g][:, t, :], ALU.mult)

        def pick_b(g, t, tag):
            picked = shared([P, PICKS], F32, tag, 1, "picked_b%d%d" % (g, t))
            nc.vector.tensor_copy(picked[:], act[g, t][:].indirect(pos2_t[:]))
            return picked

        def quantise(rounded, width, name):
            codes = held([P, width], U32, name + "_codes")
            scales = held([P, width], U8, name + "_sc")
            step = width if width == BANK else width // 2
            for c0 in range(0, width, step):
                nc.vector.quantize_mx(
                    codes[:, c0 : c0 + step].bitcast(FP8X4), scales[:, c0 : c0 + step],
                    rounded[:, PACK * c0 : PACK * (c0 + step)],
                )
            return codes, scales

        def weave(rows, copy, tag, name):
            rounded = shared([P, PACK * rows.shape[2]], BF16, tag, 1, name)
            copy(out=woven(rounded), in_=by_rows(rows))
            return rounded

        def round_xb(rows, g, t, picked):
            nc.vector.scalar_tensor_tensor(
                rows[:, t, :], picked[:], gain_t[:, g, t : t + 1], level_t[g][:, t, :], ALU.mult, ALU.max
            )

        xb_rows = held([P, PACK, PICKS], BF16, "xb_rows0")
        for t in range(PACK):
            picked = pick_b(0, t, "picked_b%d" % (t % 2))
            pick_a(0, t)
            round_xb(xb_rows, 0, t, picked)
        for t in range(PACK):
            pick_a(1, t)
        wm_bf = [weave(wm_raw[0], nc.scalar.copy, "wm_bf0", "wm_bf0")]
        xb_bf0 = weave(xb_rows, nc.scalar.copy, "xb_bf0", "xb_bf0")
        xa_bf0 = weave(picked_a[0], nc.scalar.copy, "xa_bf0", "xa_bf0")
        xa_bf1 = weave(picked_a[1], nc.scalar.copy, "xa_bf1", "xa_bf1")
        wm_bf.append(weave(wm_raw[1], nc.scalar.copy, "wm_bf1", "wm_bf1"))

        picked = [pick_b(1, 0, "factor1")]
        xb = [quantise(xb_bf0, PICKS, "xb0")]
        xa = [quantise(xa_bf0, PICKS, "xa0")]
        picked.append(pick_b(1, 1, "xa_bf0"))
        xb_rows = shared([P, PACK, PICKS], BF16, "xb_bf0", 1, "xb_rows1")
        round_xb(xb_rows, 1, 0, picked[0])
        xa.append(quantise(xa_bf1, PICKS, "xa1"))
        round_xb(xb_rows, 1, 1, picked[1])
        picked.append(pick_b(1, 2, "xa_bf1"))
        wm_q = [quantise(wm_bf[0], N, "wm0")]
        picked.append(pick_b(1, 3, "wm_bf0"))
        round_xb(xb_rows, 1, 2, picked[2])
        round_xb(xb_rows, 1, 3, picked[3])
        xb_bf1 = weave(xb_rows, nc.vector.tensor_copy, "xb_bf1", "xb_bf1")
        wm_q.append(quantise(wm_bf[1], N, "wm1"))
        xb.append(quantise(xb_bf1, PICKS, "xb1"))

        ya = shared([P, OUT_TILES, PICKS], F32, "big%d" % VIAL, 1, "ya")
        for u in range(OUT_TILES):
            acc = new_bank("ya%d" % u)
            for g in range(GROUPS):
                nc.tensor.matmul_mx(
                    out=acc[:],
                    lhsT=wx_t[:, g, 2 * u * P : 2 * (u + 1) * P].bitcast(FP4X4),
                    lhsT_scale=wx_sc[:, g, u * P : (u + 1) * P],
                    rhs=xa[g][0][:].bitcast(FP8X4), rhs_scale=xa[g][1][:],
                    start=(g == 0), stop=(g == GROUPS - 1),
                )
            nc.scalar.copy(out=ya[:, u, :], in_=acc[:])
        for u in range(OUT_TILES):
            acc = new_bank("yb%d" % u)
            for g in range(GROUPS):
                nc.tensor.matmul_mx(
                    out=acc[:],
                    lhsT=wm_q[g][0][:, u * P : (u + 1) * P].bitcast(FP8X4),
                    lhsT_scale=wm_q[g][1][:, u * P : (u + 1) * P],
                    rhs=xb[g][0][:].bitcast(FP8X4), rhs_scale=xb[g][1][:],
                    start=(g == 0), stop=(g == GROUPS - 1),
                )
            nc.vector.scalar_tensor_tensor(ya[:, u, :], acc[:], b2_t[:, u : u + 1], ya[:, u, :], ALU.add, ALU.max)
            nc.sync.dma_start(out=out[u * P : (u + 1) * P, :], in_=ya[:, u, :])
